import numpy as np
import ml_dtypes


def mxq(x, axis, fmt="e4m3"):
    dtype, down = {"e4m3": (ml_dtypes.float8_e4m3fn, 7), "e5m2": (ml_dtypes.float8_e5m2, 14)}[fmt]
    v = np.moveaxis(np.asarray(x, np.float32).astype(ml_dtypes.bfloat16).astype(np.float64), axis, -1)
    blocks = v.reshape(v.shape[:-1] + (-1, 32))
    amax = np.abs(blocks).max(-1, keepdims=True)
    byte = np.maximum(np.where(amax > 0, np.frexp(amax)[1] - 1 + 127, 0) - down, 1)
    scale = np.exp2(byte - 127.0)
    codes = (blocks / scale).astype(np.float32).astype(dtype).astype(np.float64)
    return np.moveaxis((codes * scale).reshape(v.shape), -1, axis)


WIDE = False


def mx_kscale(k):
    if not WIDE:
        return np.ones(k)
    levels = np.array([10, -10, 5, -5, 0])
    if k % 512:
        return np.exp2(np.random.permutation(np.resize(levels, k // 32))).repeat(32)
    a = np.empty((k // 512, 16))
    for p in range(k // 512):
        a[p, :8] = np.random.permutation(np.resize(levels, 8))
        for g in range(8):
            far = levels[np.abs(levels - a[p, g]) >= 10]
            a[p, g + 8] = far[np.random.randint(len(far))]
    return np.exp2(a.ravel()).repeat(32)


def f64(x):
    return np.asarray(x).astype(np.float64)


def striped8(idx):
    return np.concatenate([x.reshape(-1, 16).T for x in idx]).astype(np.uint16)


def runs(offs, k):
    lists = np.stack([offs[16 * r : 16 * r + 16].T.reshape(-1) for r in range(8)]).astype(np.int64)
    return lists[np.arange(k) % 512 // 64]


def pack_weight(w):
    k, n = w.shape
    w = f64(np.asarray(w, np.float32).astype(ml_dtypes.bfloat16)).reshape(k // 32, 32, n)
    amax = np.abs(w).max(1)
    byte = np.clip(np.where(amax > 0, np.frexp(amax)[1] - 1 + 127 - 7, 1), 1, 254)
    scaled = (w * np.exp2(127.0 - byte)[:, None, :]).reshape(k, n).astype(np.float32)
    words = np.ascontiguousarray(scaled.reshape(k // 512, 128, 4, n).transpose(0, 1, 3, 2)).astype(ml_dtypes.float8_e4m3fn).view(np.uint8)
    return words, np.ascontiguousarray(byte.astype(np.uint8).reshape(k // 512, 16, n))


def unpack_weight(words, scales):
    g, p, n, _ = words.shape
    vals = np.ascontiguousarray(words).view(ml_dtypes.float8_e4m3fn).astype(np.float64) * np.repeat(np.exp2(scales.astype(np.float64) - 127.0), 8, axis=1)[..., None]
    return vals.transpose(0, 1, 3, 2).reshape(g * 512, n)


E2M1 = np.array([0.0, 0.5, 1.0, 1.5, 2.0, 3.0, 4.0, 6.0, -0.0, -0.5, -1.0, -1.5, -2.0, -3.0, -4.0, -6.0])


def pack_fp4(w):
    k, n = w.shape
    w = f64(np.asarray(w, np.float32).astype(ml_dtypes.bfloat16)).reshape(k // 32, 32, n)
    amax = np.abs(w).max(1)
    mant, ex = np.frexp(amax / 6.0)
    byte = np.clip(np.where(amax > 0, np.where(mant > 0.5, ex, ex - 1) + 127, 1), 1, 254)
    scaled = (w * np.exp2(127.0 - byte)[:, None, :]).reshape(k, n).astype(np.float32)
    c = np.ascontiguousarray(scaled.reshape(k // 512, 128, 4, n).transpose(0, 1, 3, 2)).astype(ml_dtypes.float4_e2m1fn).view(np.uint8) & 0xF
    words = (c[..., 0::2] | (c[..., 1::2] << 4)).reshape(k // 512, 128, 2 * n)
    return np.ascontiguousarray(words), np.ascontiguousarray(byte.astype(np.uint8).reshape(k // 512, 16, n))


def unpack_fp4(words, scales):
    g, _, n = scales.shape
    words = np.ascontiguousarray(words).reshape(g, 128, n, 2)
    nib = np.empty((g, 128, n, 4), np.uint8)
    nib[..., 0::2] = words & 0xF
    nib[..., 1::2] = words >> 4
    vals = E2M1[nib] * np.repeat(np.exp2(scales.astype(np.float64) - 127.0), 8, axis=1)[..., None]
    return vals.transpose(0, 1, 3, 2).reshape(g * 512, n)


def sigmoid(v):
    return 1.0 / (1.0 + np.exp(-np.maximum(v, -700.0)))

def planes(y):
    n, m = y.shape
    v = y.astype(np.float32).astype(ml_dtypes.bfloat16).astype(np.float64).reshape(n // 32, 32, m)
    top = np.abs(v).max(1)
    byte = np.clip(np.where(top > 0, np.frexp(top)[1] - 1 + 127 - 7, 1), 1, 254)
    codes = (v * np.exp2(127.0 - byte)[:, None, :]).reshape(n, m).astype(np.float32).astype(ml_dtypes.float8_e4m3fn).view(np.uint8)
    words = codes.reshape(n // 512, 128, 4, m).transpose(0, 1, 3, 2)
    return np.ascontiguousarray(words), np.ascontiguousarray(byte.astype(np.uint8).reshape(n // 512, 16, m))


K, T, S, N, H = 512, 2048, 512, 512, 512


def setup_inputs():
    n = np.random.standard_normal
    s = mx_kscale(K)[:, None]
    u = mx_kscale(H)
    packed_xT = pack_weight(n((K, T)) * s)
    packed_w1 = pack_fp4(n((K, H)) / np.sqrt(K) / s)
    packed_w2 = pack_fp4(n((H, N)) / np.sqrt(H) / u[:, None])
    return {
        "x_words": packed_xT[0],
        "x_scales": packed_xT[1],
        "w1_words": packed_w1[0],
        "w1_scales": packed_w1[1],
        "gn": (np.random.uniform(0.5, 1.5, (H, 1)) * u[:, None]).astype(np.float32),
        "w2_words": packed_w2[0],
        "w2_scales": packed_w2[1],
        "offs": striped8(np.random.randint(0, T, (8, S))),
        "n1": striped8(np.stack([np.random.permutation(S) for _ in range(8)])),
        "n2": striped8(np.stack([np.random.permutation(S) for _ in range(8)])),
        "n3": striped8(np.stack([np.random.permutation(S) for _ in range(8)])),
        "n4": striped8(np.stack([np.random.permutation(S) for _ in range(8)])),
    }


def reference(x_words, x_scales, w1_words, w1_scales, gn, w2_words, w2_scales, offs, n1, n2, n3, n4):
    xq = unpack_weight(x_words, x_scales)[np.arange(K)[:, None], runs(offs, K)]
    y = unpack_fp4(w1_words, w1_scales).T @ xq
    z = f64(gn) * (np.maximum(y * (sigmoid(y[np.arange(H)[:, None], runs(n1, H)])), y[np.arange(H)[:, None], runs(n2, H)]))
    h = unpack_fp4(w2_words, w2_scales).T @ mxq(z, 0, "e4m3")
    out_0 = (h[np.arange(N)[:, None], runs(n3, N)]) / (np.abs(h) + np.abs(h[np.arange(N)[:, None], runs(n4, N)]) + 0.5)
    return (out_0,) + planes(out_0)

@@ -1,0 +1,263 @@
+from contextlib import ExitStack
+
+import concourse.mybir as mybir
+
+K, T, S, N, H = 512, 2048, 512, 512, 512
+FLOPS = 2 * K * H * S + 2 * H * N * S
+
+F32 = mybir.dt.float32
+BF16 = mybir.dt.bfloat16
+I32 = mybir.dt.int32
+U32 = mybir.dt.uint32
+U16 = mybir.dt.uint16
+U8 = mybir.dt.uint8
+FP8X4 = mybir.dt.float8_e4m3fn_x4
+FP4X4 = mybir.dt.float4_e2m1fn_x4
+ALU = mybir.AluOpType
+ACT = mybir.ActivationFunctionType
+
+P = 128
+PACK = 4
+HALF = S // 2
+GROUP = 16
+
+
+def tile_picked_hashgmaxnorm2_none_po_kernel(
+    tc, x_words, x_scales, w1_words, w1_scales, gn, w2_words, w2_scales, offs, n1, n2, n3, n4, out_0, out_1, out_2
+):
+    nc = tc.nc
+    with ExitStack() as ctx:
+        held = ctx.enter_context(tc.tile_pool(name="held", bufs=1))
+        psum = ctx.enter_context(tc.psum_pool(name="psum", bufs=1))
+
+        def sb(name, shape, dtype):
+            return held.tile(shape, dtype, name=name, align_bytes=64)
+
+        def cols(c):
+            return slice(c * HALF, (c + 1) * HALF)
+
+        def entries(lst, c):
+            return lst[:, c * HALF // GROUP : (c + 1) * HALF // GROUP]
+
+        lists = {}
+        for name in ("offs", "n1", "n2", "n3", "n4"):
+            lists[name] = held.tile([P, S // GROUP], U16, name="list_" + name)
+
+        x_table = sb("x_table", [P, T], I32)
+        xs_table = sb("xs_table", [P, T], U8)
+        x_picked = sb("x_picked", [P, S], U32)
+        xs_picked = sb("xs_picked", [P, S], U8)
+        xs_plane = sb("xs_plane", [P, S], U8)
+        w_raw = sb("w_raw", [P, 2 * H], U8)
+        ws_raw = sb("ws_raw", [P, H], U8)
+        w1_dealt = sb("w1_dealt", [P, 2 * H], U8)
+        w2_dealt = sb("w2_dealt", [P, 2 * N], U8)
+        w1s_dealt = sb("w1s_dealt", [P, H], U8)
+        w2s_dealt = sb("w2s_dealt", [P, N], U8)
+        gain = sb("gain", [P, PACK], F32)
+
+        def load_scale_rows(src):
+            for q in range(4):
+                nc.sync.dma_start(ws_raw[32 * q : 32 * q + 4, :].bitcast(I32), src[0, 4 * q : 4 * q + 4, :].bitcast(I32))
+
+        def deal_words(dst):
+            nc.scalar.copy(
+                dst[:].bitcast(U16).rearrange("p (t m) -> p t m", t=PACK),
+                w_raw[:].bitcast(U16).rearrange("p (m t) -> p t m", t=PACK),
+            )
+
+        def deal_scales(dst):
+            nc.vector.tensor_copy(
+                dst[:].rearrange("p (t m) -> p t m", t=PACK), ws_raw[:].rearrange("p (m t) -> p t m", t=PACK)
+            )
+
+        nc.vector.memset(xs_table[:].bitcast(I32), 0)
+        nc.vector.memset(ws_raw[:].bitcast(I32), 0)
+        nc.vector.memset(xs_plane[:].bitcast(I32), 0)
+        nc.sync.dma_start(lists["offs"][:], offs)
+        nc.sync.dma_start(xs_table[0:P:8, :].bitcast(I32), x_scales[0].bitcast(I32))
+        nc.scalar.dma_start(x_table[:], x_words[0].rearrange("p n t -> p (n t)").bitcast(I32))
+        load_scale_rows(w1_scales)
+        nc.scalar.dma_start(w_raw[:].bitcast(I32), w1_words[0].bitcast(I32))
+        nc.sync.dma_start(lists["n1"][:], n1)
+        nc.sync.dma_start(lists["n2"][:], n2)
+        nc.sync.dma_start(lists["n3"][:], n3)
+        nc.sync.dma_start(lists["n4"][:], n4)
+        nc.gpsimd.dma_start(gain[:], gn.rearrange("(p t) o -> p (t o)", t=PACK))
+
+        nc.vector.tensor_copy(xs_picked[:], xs_table[:].indirect(lists["offs"][:]))
+        deal_words(w1_dealt)
+        for j in range(4):
+            nc.scalar.dma_start(xs_plane[j:P:32, :].bitcast(I32), xs_picked[8 * j : P : 32, :].bitcast(I32))
+        deal_scales(w1s_dealt)
+        nc.vector.tensor_copy(x_picked[:], x_table[:].bitcast(U32).indirect(lists["offs"][:]))
+        nc.sync.dma_start(w_raw[:].bitcast(I32), w2_words[0].bitcast(I32))
+        load_scale_rows(w2_scales)
+
+        def product(out, words, scales, t, codes, plane):
+            nc.tensor.matmul_mx(
+                out=out,
+                lhsT=words[:, 2 * P * t : 2 * P * (t + 1)].bitcast(FP4X4),
+                lhsT_scale=scales[:, P * t : P * (t + 1)],
+                rhs=codes.bitcast(FP8X4),
+                rhs_scale=plane,
+                start=True,
+                stop=True,
+            )
+
+        def bank(b):
+            return psum.tile([P, S], F32, name="bank%d" % b, tag="bank%d" % b)
+
+        y = [sb("y%d" % t, [P, S], F32) for t in range(PACK)]
+        sig = [sb("sig%d" % t, [P, S], F32) for t in range(PACK)]
+        gated = [sb("gated%d" % c, [P, PACK, HALF], F32) for c in range(2)]
+        other = [sb("other%d" % c, [P, PACK, HALF], F32) for c in range(2)]
+        larger = [sb("larger%d" % c, [P, PACK, HALF], F32) for c in range(2)]
+        z_bf = [sb("z_bf%d" % c, [P, HALF, PACK], BF16) for c in range(2)]
+        z_codes = [sb("z_codes%d" % c, [P, HALF], U32) for c in range(2)]
+        z_plane = [sb("z_plane%d" % c, [P, HALF], U8) for c in range(2)]
+
+        y0_banks = [bank(0), bank(4)]
+        for c in range(2):
+            product(y0_banks[c][:, :HALF], w1_dealt, w1s_dealt, 0, x_picked[:, cols(c)], xs_plane[:, cols(c)])
+        y_banks = [None]
+        for t in range(1, PACK):
+            y_banks.append(bank(t))
+            product(y_banks[t][:], w1_dealt, w1s_dealt, t, x_picked[:], xs_plane[:])
+        for c in range(2):
+            nc.scalar.activation(sig[0][:, cols(c)], y0_banks[c][:, :HALF], ACT.Sigmoid)
+            nc.vector.tensor_copy(y[0][:, cols(1 - c)], y0_banks[1 - c][:, :HALF])
+
+        def gate(t, c):
+            nc.vector.tensor_tensor(
+                gated[c][:, t, :], sig[t][:].indirect(entries(lists["n1"], c)), y[t][:, cols(c)], ALU.mult
+            )
+
+        def fetch_other(t, c):
+            nc.scalar.activation(other[c][:, t, :], y[t][:].indirect(entries(lists["n2"], c)), ACT.Copy)
+
+        def take_larger(t, c):
+            nc.vector.tensor_tensor(larger[c][:, t, :], gated[c][:, t, :], other[c][:, t, :], ALU.max)
+
+        def scale_and_round(c):
+            nc.vector.tensor_tensor(
+                z_bf[c][:].rearrange("p (g i) t -> p g t i", i=4),
+                larger[c][:].rearrange("p t (g i) -> p g t i", i=4),
+                gain[:].unsqueeze(1).unsqueeze(3).to_broadcast([P, HALF // 4, PACK, 4]),
+                ALU.mult,
+            )
+
+        def quantize_z(c):
+            nc.vector.quantize_mx(
+                out=z_codes[c][:].bitcast(FP8X4), scales=z_plane[c][:], in_=z_bf[c][:].rearrange("p j t -> p (j t)")
+            )
+
+        for t in range(PACK):
+            if t > 0:
+                nc.scalar.copy(y[t][:], y_banks[t][:])
+                nc.scalar.activation(sig[t][:], y_banks[t][:], ACT.Sigmoid)
+            for c in range(2):
+                gate(t, c)
+        for c in range(2):
+            for t in range(PACK):
+                fetch_other(t, c)
+        deal_words(w2_dealt)
+        deal_scales(w2s_dealt)
+
+        h = [sb("h%d" % t, [P, S], F32) for t in range(PACK)]
+        size = [sb("size%d" % t, [P, S], F32) for t in range(PACK)]
+        part = [sb("part%d" % c, [P, PACK, HALF], F32) for c in range(2)]
+        total = [sb("total%d" % c, [P, PACK, HALF], F32) for c in range(2)]
+        root = [sb("root%d" % c, [P, PACK, HALF], F32) for c in range(2)]
+        inverse = [sb("inverse%d" % c, [P, PACK, HALF], F32) for c in range(2)]
+        result = [sb("result%d" % c, [P, PACK, HALF], F32) for c in range(2)]
+        out_bf = [sb("out_bf%d" % c, [P, HALF, PACK], BF16) for c in range(2)]
+        out_codes = sb("out_codes", [P, S], U32)
+        out_plane = sb("out_plane", [P, S], U8)
+
+        h_banks = {}
+
+        def second_product(c):
+            for t in range(PACK):
+                h_banks[t, c] = bank(t + 4 * (1 - c))
+                product(h_banks[t, c][:, :HALF], w2_dealt, w2s_dealt, t, z_codes[c][:], z_plane[c][:])
+
+        for t in range(PACK):
+            take_larger(t, 0)
+        scale_and_round(0)
+        take_larger(0, 1)
+        quantize_z(0)
+        second_product(0)
+        for t in range(PACK):
+            nc.scalar.activation(size[t][:, cols(0)], h_banks[t, 0][:, :HALF], ACT.Abs)
+        for t in range(1, PACK):
+            take_larger(t, 1)
+        nc.vector.tensor_copy(h[0][:, cols(0)], h_banks[0, 0][:, :HALF])
+        scale_and_round(1)
+        nc.vector.tensor_copy(h[1][:, cols(0)], h_banks[1, 0][:, :HALF])
+        quantize_z(1)
+        second_product(1)
+        for t in range(PACK - 1):
+            nc.scalar.activation(part[0][:, t, :], h_banks[t, 0][:, :HALF], ACT.Abs)
+        for t in range(2, PACK):
+            nc.vector.tensor_copy(h[t][:, cols(0)], h_banks[t, 0][:, :HALF])
+
+        out_rows = out_0.rearrange("(p t) j -> p t j", t=PACK)
+
+        def add_sizes(t, c):
+            if t < PACK - 1:
+                nc.vector.tensor_tensor(
+                    total[c][:, t, :], size[t][:].indirect(entries(lists["n4"], c)), part[c][:, t, :], ALU.add
+                )
+            else:
+                nc.scalar.activation(part[c][:, t, :], size[t][:].indirect(entries(lists["n4"], c)), ACT.Copy)
+                nc.vector.tensor_tensor(total[c][:, t, :], part[c][:, t, :], size[t][:, cols(c)], ALU.add)
+
+        def invert(t, c):
+            nc.scalar.activation(root[c][:, t, :], total[c][:, t, :], ACT.Abs_reciprocal_sqrt, bias=0.5)
+            nc.scalar.activation(inverse[c][:, t, :], root[c][:, t, :], ACT.Square)
+
+        def divide(t, c):
+            nc.vector.tensor_tensor(
+                result[c][:, t, :], h[t][:].indirect(entries(lists["n3"], c)), inverse[c][:, t, :], ALU.mult
+            )
+            nc.sync.dma_start(out_rows[:, t, cols(c)], result[c][:, t, :])
+
+        def round_out(c):
+            nc.vector.tensor_copy(
+                out_bf[c][:].rearrange("p (g i) t -> p g t i", i=4), result[c][:].rearrange("p t (g i) -> p g t i", i=4)
+            )
+
+        def quantize_out(c):
+            nc.vector.quantize_mx(
+                out=out_codes[:, cols(c)].bitcast(FP8X4),
+                scales=out_plane[:, cols(c)],
+                in_=out_bf[c][:].rearrange("p j t -> p (j t)"),
+            )
+            nc.sync.dma_start(
+                out_1[0].rearrange("p n t -> p (n t)").bitcast(I32)[:, cols(c)], out_codes[:, cols(c)].bitcast(I32)
+            )
+
+        for t in range(PACK):
+            nc.scalar.activation(size[t][:, cols(1)], h_banks[t, 1][:, :HALF], ACT.Abs)
+            add_sizes(t, 0)
+            if t < PACK - 1:
+                nc.scalar.activation(part[1][:, t, :], h_banks[t, 1][:, :HALF], ACT.Abs)
+            nc.scalar.copy(h[t][:, cols(1)], h_banks[t, 1][:, :HALF])
+        for t in range(PACK):
+            invert(t, 0)
+            add_sizes(t, 1)
+        for t in range(PACK):
+            divide(t, 0)
+            invert(t, 1)
+        divide(0, 1)
+        round_out(0)
+        divide(1, 1)
+        quantize_out(0)
+        divide(2, 1)
+        divide(3, 1)
+        round_out(1)
+        quantize_out(1)
+        for q in range(4):
+            queue = nc.sync if q % 2 == 0 else nc.scalar
+            queue.dma_start(out_2[0, 4 * q : 4 * q + 4, :].bitcast(I32), out_plane[32 * q : 32 * q + 4, :].bitcast(I32))

@@ -1,6 +1,7 @@
 from contextlib import ExitStack
 
 import concourse.mybir as mybir
+from concourse.masks import make_identity
 
 K, T, S, N, H = 512, 2048, 512, 512, 512
 FLOPS = 2 * K * H * S + 2 * H * N * S
@@ -20,6 +21,10 @@ P = 128
 PACK = 4
 HALF = S // 2
 GROUP = 16
+G = 1
+H_ON_VECTOR = []
+WARM = True
+ON_SCALAR = [(3, 1)]
 
 
 def tile_picked_hashgmaxnorm2_none_po_kernel(
@@ -30,8 +35,8 @@ def tile_picked_hashgmaxnorm2_none_po_kernel(
         held = ctx.enter_context(tc.tile_pool(name="held", bufs=1))
         psum = ctx.enter_context(tc.psum_pool(name="psum", bufs=1))
 
-        def sb(name, shape, dtype):
-            return held.tile(shape, dtype, name=name, align_bytes=64)
+        def sb(name, shape, dtype, tag=None):
+            return held.tile(shape, dtype, name=name, tag=tag or name, align_bytes=64)
 
         def cols(c):
             return slice(c * HALF, (c + 1) * HALF)
@@ -51,48 +56,61 @@ def tile_picked_hashgmaxnorm2_none_po_kernel(
         w_raw = sb("w_raw", [P, 2 * H], U8)
         ws_raw = sb("ws_raw", [P, H], U8)
         w1_dealt = sb("w1_dealt", [P, 2 * H], U8)
-        w2_dealt = sb("w2_dealt", [P, 2 * N], U8)
         w1s_dealt = sb("w1s_dealt", [P, H], U8)
-        w2s_dealt = sb("w2s_dealt", [P, N], U8)
         gain = sb("gain", [P, PACK], F32)
 
-        def load_scale_rows(src):
-            for q in range(4):
-                nc.sync.dma_start(ws_raw[32 * q : 32 * q + 4, :].bitcast(I32), src[0, 4 * q : 4 * q + 4, :].bitcast(I32))
+        w2_raw = sb("w2_raw", [P, 2 * N], U8)
+        identity = sb("identity", [P, P], F32)
 
-        def deal_words(dst):
+        w2_dealt = sb("w2_dealt", [P, 2 * N], U8)
+        ws2_raw = sb("ws2_raw", [P, N], U8)
+        w2s_dealt = sb("w2s_dealt", [P, N], U8)
+
+        def load_scale_rows(queue, raw, src):
+            for q in range(4):
+                queue.dma_start(raw[32 * q : 32 * q + 4, :].bitcast(I32), src[0, 4 * q : 4 * q + 4, :].bitcast(I32))
+
+        def deal_words(dst, raw):
             nc.scalar.copy(
                 dst[:].bitcast(U16).rearrange("p (t m) -> p t m", t=PACK),
-                w_raw[:].bitcast(U16).rearrange("p (m t) -> p t m", t=PACK),
+                raw[:].bitcast(U16).rearrange("p (m t) -> p t m", t=PACK),
             )
 
-        def deal_scales(dst):
-            nc.vector.tensor_copy(
-                dst[:].rearrange("p (t m) -> p t m", t=PACK), ws_raw[:].rearrange("p (m t) -> p t m", t=PACK)
+        def deal_scales(engine, dst, raw):
+            engine.tensor_copy(
+                dst[:].rearrange("p (t m) -> p t m", t=PACK), raw[:].rearrange("p (m t) -> p t m", t=PACK)
             )
 
         nc.vector.memset(xs_table[:].bitcast(I32), 0)
         nc.vector.memset(ws_raw[:].bitcast(I32), 0)
         nc.vector.memset(xs_plane[:].bitcast(I32), 0)
         nc.sync.dma_start(lists["offs"][:], offs)
-        nc.sync.dma_start(xs_table[0:P:8, :].bitcast(I32), x_scales[0].bitcast(I32))
-        nc.scalar.dma_start(x_table[:], x_words[0].rearrange("p n t -> p (n t)").bitcast(I32))
-        load_scale_rows(w1_scales)
-        nc.scalar.dma_start(w_raw[:].bitcast(I32), w1_words[0].bitcast(I32))
+        nc.scalar.dma_start(xs_table[0:P:8, :].bitcast(I32), x_scales[0].bitcast(I32))
+        load_scale_rows(nc.scalar, ws_raw, w1_scales)
         nc.sync.dma_start(lists["n1"][:], n1)
         nc.sync.dma_start(lists["n2"][:], n2)
         nc.sync.dma_start(lists["n3"][:], n3)
         nc.sync.dma_start(lists["n4"][:], n4)
+        nc.sync.dma_start(x_table[:], x_words[0].rearrange("p n t -> p (n t)").bitcast(I32))
+        nc.gpsimd.dma_start(w_raw[:].bitcast(I32), w1_words[0].bitcast(I32))
+        nc.gpsimd.dma_start(w2_raw[:].bitcast(I32), w2_words[0].bitcast(I32))
+        nc.gpsimd.memset(ws2_raw[:].bitcast(I32), 0)
+        load_scale_rows(nc.gpsimd, ws2_raw, w2_scales)
         nc.gpsimd.dma_start(gain[:], gn.rearrange("(p t) o -> p (t o)", t=PACK))
+        make_identity(nc, identity[:])
+        warm = sb("warm", [P, 3], F32)
+        if WARM:
+            nc.vector.memset(warm[:, 0:1], 0.0)
+            nc.scalar.activation(warm[:, 1:2], warm[:, 0:1], ACT.Sigmoid)
 
         nc.vector.tensor_copy(xs_picked[:], xs_table[:].indirect(lists["offs"][:]))
-        deal_words(w1_dealt)
         for j in range(4):
-            nc.scalar.dma_start(xs_plane[j:P:32, :].bitcast(I32), xs_picked[8 * j : P : 32, :].bitcast(I32))
-        deal_scales(w1s_dealt)
+            nc.sync.dma_start(xs_plane[j:P:32, :].bitcast(I32), xs_picked[8 * j : P : 32, :].bitcast(I32))
+        deal_words(w1_dealt, w_raw)
         nc.vector.tensor_copy(x_picked[:], x_table[:].bitcast(U32).indirect(lists["offs"][:]))
-        nc.sync.dma_start(w_raw[:].bitcast(I32), w2_words[0].bitcast(I32))
-        load_scale_rows(w2_scales)
+        deal_scales(nc.vector, w1s_dealt, ws_raw)
+        deal_words(w2_dealt, w2_raw)
+        deal_scales(nc.gpsimd, w2s_dealt, ws2_raw)
 
         def product(out, words, scales, t, codes, plane):
             nc.tensor.matmul_mx(
@@ -112,7 +130,7 @@ def tile_picked_hashgmaxnorm2_none_po_kernel(
         sig = [sb("sig%d" % t, [P, S], F32) for t in range(PACK)]
         gated = [sb("gated%d" % c, [P, PACK, HALF], F32) for c in range(2)]
         other = [sb("other%d" % c, [P, PACK, HALF], F32) for c in range(2)]
-        larger = [sb("larger%d" % c, [P, PACK, HALF], F32) for c in range(2)]
+        larger = [sb("larger1", [P, PACK, HALF], F32)] * 2
         z_bf = [sb("z_bf%d" % c, [P, HALF, PACK], BF16) for c in range(2)]
         z_codes = [sb("z_codes%d" % c, [P, HALF], U32) for c in range(2)]
         z_plane = [sb("z_plane%d" % c, [P, HALF], U8) for c in range(2)]
@@ -136,8 +154,9 @@ def tile_picked_hashgmaxnorm2_none_po_kernel(
         def fetch_other(t, c):
             nc.scalar.activation(other[c][:, t, :], y[t][:].indirect(entries(lists["n2"], c)), ACT.Copy)
 
-        def take_larger(t, c):
-            nc.vector.tensor_tensor(larger[c][:, t, :], gated[c][:, t, :], other[c][:, t, :], ALU.max)
+        def take_larger(pair, c):
+            ts = slice(2 * pair, 2 * pair + 2)
+            nc.vector.tensor_tensor(larger[c][:, ts, :], gated[c][:, ts, :], other[c][:, ts, :], ALU.max)
 
         def scale_and_round(c):
             nc.vector.tensor_tensor(
@@ -156,18 +175,19 @@ def tile_picked_hashgmaxnorm2_none_po_kernel(
             if t > 0:
                 nc.scalar.copy(y[t][:], y_banks[t][:])
                 nc.scalar.activation(sig[t][:], y_banks[t][:], ACT.Sigmoid)
-            for c in range(2):
-                gate(t, c)
-        for c in range(2):
-            for t in range(PACK):
-                fetch_other(t, c)
-        deal_words(w2_dealt)
-        deal_scales(w2s_dealt)
+                fetch_other(t - 1, 0)
+            gate(t, 0)
+            if t < PACK - 1:
+                gate(t, 1)
+        fetch_other(PACK - 1, 0)
+        for t in range(PACK):
+            fetch_other(t, 1)
+        if WARM:
+            nc.scalar.activation(warm[:, 2:3], other[1][:, PACK - 1, 0:1], ACT.Abs_reciprocal_sqrt, bias=0.5, scale=0.0)
 
-        h = [sb("h%d" % t, [P, S], F32) for t in range(PACK)]
+        h = [sb("h%d" % t, [P, S], F32) for t in range(2)]
         size = [sb("size%d" % t, [P, S], F32) for t in range(PACK)]
-        part = [sb("part%d" % c, [P, PACK, HALF], F32) for c in range(2)]
-        total = [sb("total%d" % c, [P, PACK, HALF], F32) for c in range(2)]
+        part = [sb("part", [P, PACK, HALF], F32)] * 2
         root = [sb("root%d" % c, [P, PACK, HALF], F32) for c in range(2)]
         inverse = [sb("inverse%d" % c, [P, PACK, HALF], F32) for c in range(2)]
         result = [sb("result%d" % c, [P, PACK, HALF], F32) for c in range(2)]
@@ -182,40 +202,65 @@ def tile_picked_hashgmaxnorm2_none_po_kernel(
                 h_banks[t, c] = bank(t + 4 * (1 - c))
                 product(h_banks[t, c][:, :HALF], w2_dealt, w2s_dealt, t, z_codes[c][:], z_plane[c][:])
 
-        for t in range(PACK):
-            take_larger(t, 0)
+        take_larger(0, 0)
+        take_larger(1, 0)
         scale_and_round(0)
-        take_larger(0, 1)
+        gate(PACK - 1, 1)
         quantize_z(0)
         second_product(0)
         for t in range(PACK):
             nc.scalar.activation(size[t][:, cols(0)], h_banks[t, 0][:, :HALF], ACT.Abs)
-        for t in range(1, PACK):
-            take_larger(t, 1)
-        nc.vector.tensor_copy(h[0][:, cols(0)], h_banks[0, 0][:, :HALF])
+        take_larger(0, 1)
+        take_larger(1, 1)
         scale_and_round(1)
-        nc.vector.tensor_copy(h[1][:, cols(0)], h_banks[1, 0][:, :HALF])
         quantize_z(1)
         second_product(1)
-        for t in range(PACK - 1):
-            nc.scalar.activation(part[0][:, t, :], h_banks[t, 0][:, :HALF], ACT.Abs)
+        h.append(sb("h2", [P, S], F32, tag="larger1"))
+        h.append(sb("h3", [P, S], F32, tag="z_bf1"))
         for t in range(2, PACK):
             nc.vector.tensor_copy(h[t][:, cols(0)], h_banks[t, 0][:, :HALF])
 
         out_rows = out_0.rearrange("(p t) j -> p t j", t=PACK)
 
-        def add_sizes(t, c):
-            if t < PACK - 1:
-                nc.vector.tensor_tensor(
-                    total[c][:, t, :], size[t][:].indirect(entries(lists["n4"], c)), part[c][:, t, :], ALU.add
-                )
+        def fetch_size(t, c):
+            window = size[t][:].indirect(entries(lists["n4"], c))
+            if (t, c) in ON_SCALAR:
+                nc.scalar.activation(part[c][:, t, :], window, ACT.Copy)
             else:
-                nc.scalar.activation(part[c][:, t, :], size[t][:].indirect(entries(lists["n4"], c)), ACT.Copy)
-                nc.vector.tensor_tensor(total[c][:, t, :], part[c][:, t, :], size[t][:, cols(c)], ALU.add)
+                nc.vector.tensor_copy(part[c][:, t, :], window)
 
-        def invert(t, c):
-            nc.scalar.activation(root[c][:, t, :], total[c][:, t, :], ACT.Abs_reciprocal_sqrt, bias=0.5)
-            nc.scalar.activation(inverse[c][:, t, :], root[c][:, t, :], ACT.Square)
+        def invert(t0, c):
+            sums = bank(4 + (t0 // G) % 2)
+            for t in range(t0, t0 + G):
+                for b in range(HALF // P):
+                    block = slice(b * P, (b + 1) * P)
+                    place = slice((t - t0) * HALF + b * P, (t - t0) * HALF + (b + 1) * P)
+                    nc.tensor.matmul(
+                        sums[:, place], part[c][:, t, block], identity[:], start=True, stop=False, is_transpose=True
+                    )
+                    nc.tensor.matmul(
+                        sums[:, place], size[t][:, cols(c)][:, block], identity[:], start=False, stop=True, is_transpose=True
+                    )
+            nc.scalar.activation(
+                root[c][:, t0 : t0 + G, :].rearrange("p t j -> p (t j)"), sums[:, : G * HALF], ACT.Abs_reciprocal_sqrt, bias=0.5
+            )
+
+        def turn_back(t0, c):
+            roots = bank(6 + (t0 // G) % 2)
+            for t in range(t0, t0 + G):
+                for b in range(HALF // P):
+                    block = slice(b * P, (b + 1) * P)
+                    place = slice((t - t0) * HALF + b * P, (t - t0) * HALF + (b + 1) * P)
+                    nc.tensor.transpose(roots[:, place], root[c][:, t, block], identity[:])
+            nc.scalar.activation(
+                inverse[c][:, t0 : t0 + G, :].rearrange("p t j -> p (t j)"), roots[:, : G * HALF], ACT.Square
+            )
+
+        def copy_h(t, c):
+            if (t, c) in H_ON_VECTOR:
+                nc.vector.tensor_copy(h[t][:, cols(c)], h_banks[t, c][:, :HALF])
+            else:
+                nc.scalar.copy(h[t][:, cols(c)], h_banks[t, c][:, :HALF])
 
         def divide(t, c):
             nc.vector.tensor_tensor(
@@ -240,22 +285,27 @@ def tile_picked_hashgmaxnorm2_none_po_kernel(
 
         for t in range(PACK):
             nc.scalar.activation(size[t][:, cols(1)], h_banks[t, 1][:, :HALF], ACT.Abs)
-            add_sizes(t, 0)
-            if t < PACK - 1:
-                nc.scalar.activation(part[1][:, t, :], h_banks[t, 1][:, :HALF], ACT.Abs)
-            nc.scalar.copy(h[t][:, cols(1)], h_banks[t, 1][:, :HALF])
-        for t in range(PACK):
-            invert(t, 0)
-            add_sizes(t, 1)
-        for t in range(PACK):
-            divide(t, 0)
-            invert(t, 1)
-        divide(0, 1)
-        round_out(0)
-        divide(1, 1)
-        quantize_out(0)
-        divide(2, 1)
-        divide(3, 1)
+            fetch_size(t, 0)
+            if t < 2:
+                copy_h(t, 0)
+        pieces = [(t, c) for c in range(2) for t in range(0, PACK, G)]
+        for step in range(len(pieces) + 2):
+            if step < len(pieces):
+                invert(*pieces[step])
+            if 1 <= step <= len(pieces):
+                turn_back(*pieces[step - 1])
+            if step < PACK // G:
+                for t in range(step * G, (step + 1) * G):
+                    copy_h(t, 1)
+                    fetch_size(t, 1)
+            if 2 <= step:
+                t0, c = pieces[step - 2]
+                for t in range(t0, t0 + G):
+                    divide(t, c)
+            if step == PACK // G + 2:
+                round_out(0)
+            if step == PACK // G + 3:
+                quantize_out(0)
         round_out(1)
         quantize_out(1)
         for q in range(4):

@@ -21,6 +21,13 @@ P = 128
 PACK = 4
 HALF = S // 2
 GROUP = 16
+ZS = 2
+Y_ON_VECTOR = []
+OTHER_ON_VECTOR = [(3, 0)]
+WARM_T = 3
+SUMS = 6
+SPLIT = 2
+ROUND0 = 0
 G = 1
 H_ON_VECTOR = []
 WARM = True
@@ -50,7 +57,6 @@ def tile_picked_hashgmaxnorm2_none_po_kernel(
 
         x_table = sb("x_table", [P, T], I32)
         xs_table = sb("xs_table", [P, T], U8)
-        x_picked = sb("x_picked", [P, S], U32)
         xs_picked = sb("xs_picked", [P, S], U8)
         xs_plane = sb("xs_plane", [P, S], U8)
         w_raw = sb("w_raw", [P, 2 * H], U8)
@@ -68,7 +74,7 @@ def tile_picked_hashgmaxnorm2_none_po_kernel(
 
         def load_scale_rows(queue, raw, src):
             for q in range(4):
-                queue.dma_start(raw[32 * q : 32 * q + 4, :].bitcast(I32), src[0, 4 * q : 4 * q + 4, :].bitcast(I32))
+                queue[q].dma_start(raw[32 * q : 32 * q + 4, :].bitcast(I32), src[0, 4 * q : 4 * q + 4, :].bitcast(I32))
 
         def deal_words(dst, raw):
             nc.scalar.copy(
@@ -83,20 +89,17 @@ def tile_picked_hashgmaxnorm2_none_po_kernel(
 
         nc.vector.memset(xs_table[:].bitcast(I32), 0)
         nc.vector.memset(ws_raw[:].bitcast(I32), 0)
-        nc.vector.memset(xs_plane[:].bitcast(I32), 0)
         nc.sync.dma_start(lists["offs"][:], offs)
-        nc.scalar.dma_start(xs_table[0:P:8, :].bitcast(I32), x_scales[0].bitcast(I32))
-        load_scale_rows(nc.scalar, ws_raw, w1_scales)
+        nc.sync.dma_start(xs_table[0:P:8, :].bitcast(I32), x_scales[0].bitcast(I32))
         nc.sync.dma_start(lists["n1"][:], n1)
         nc.sync.dma_start(lists["n2"][:], n2)
-        nc.sync.dma_start(lists["n3"][:], n3)
-        nc.sync.dma_start(lists["n4"][:], n4)
         nc.sync.dma_start(x_table[:], x_words[0].rearrange("p n t -> p (n t)").bitcast(I32))
+        load_scale_rows([nc.scalar] * 4, ws_raw, w1_scales)
         nc.gpsimd.dma_start(w_raw[:].bitcast(I32), w1_words[0].bitcast(I32))
+        nc.gpsimd.dma_start(gain[:], gn.rearrange("(p t) o -> p (t o)", t=PACK))
         nc.gpsimd.dma_start(w2_raw[:].bitcast(I32), w2_words[0].bitcast(I32))
         nc.gpsimd.memset(ws2_raw[:].bitcast(I32), 0)
-        load_scale_rows(nc.gpsimd, ws2_raw, w2_scales)
-        nc.gpsimd.dma_start(gain[:], gn.rearrange("(p t) o -> p (t o)", t=PACK))
+        load_scale_rows([nc.gpsimd] * 4, ws2_raw, w2_scales)
         make_identity(nc, identity[:])
         warm = sb("warm", [P, 3], F32)
         if WARM:
@@ -104,11 +107,19 @@ def tile_picked_hashgmaxnorm2_none_po_kernel(
             nc.scalar.activation(warm[:, 1:2], warm[:, 0:1], ACT.Sigmoid)
 
         nc.vector.tensor_copy(xs_picked[:], xs_table[:].indirect(lists["offs"][:]))
-        for j in range(4):
+        nc.vector.tensor_copy(xs_plane[:].bitcast(I32), xs_picked[:].bitcast(I32))
+        for j in range(1, 4):
             nc.sync.dma_start(xs_plane[j:P:32, :].bitcast(I32), xs_picked[8 * j : P : 32, :].bitcast(I32))
+        nc.sync.dma_start(lists["n3"][:], n3)
+        nc.sync.dma_start(lists["n4"][:], n4)
         deal_words(w1_dealt, w_raw)
-        nc.vector.tensor_copy(x_picked[:], x_table[:].bitcast(U32).indirect(lists["offs"][:]))
+        gain_size = sb("gain_size", [P, PACK], F32)
+        gain_sign = sb("gain_sign", [P, HALF, PACK], BF16)
+        nc.scalar.activation(gain_size[:], gain[:], ACT.Abs)
+        nc.scalar.activation(gain_sign[:], gain[:].unsqueeze(1).to_broadcast([P, HALF, PACK]), ACT.Sign)
         deal_scales(nc.vector, w1s_dealt, ws_raw)
+        x_picked = sb("x_picked", [P, S], U32, tag="ws_raw")
+        nc.vector.tensor_copy(x_picked[:], x_table[:].bitcast(U32).indirect(lists["offs"][:]))
         deal_words(w2_dealt, w2_raw)
         deal_scales(nc.gpsimd, w2s_dealt, ws2_raw)
 
@@ -130,7 +141,7 @@ def tile_picked_hashgmaxnorm2_none_po_kernel(
         sig = [sb("sig%d" % t, [P, S], F32) for t in range(PACK)]
         gated = [sb("gated%d" % c, [P, PACK, HALF], F32) for c in range(2)]
         other = [sb("other%d" % c, [P, PACK, HALF], F32) for c in range(2)]
-        larger = [sb("larger1", [P, PACK, HALF], F32)] * 2
+        larger = [sb("larger1", [P, HALF, PACK], BF16)] * 2
         z_bf = [sb("z_bf%d" % c, [P, HALF, PACK], BF16) for c in range(2)]
         z_codes = [sb("z_codes%d" % c, [P, HALF], U32) for c in range(2)]
         z_plane = [sb("z_plane%d" % c, [P, HALF], U8) for c in range(2)]
@@ -144,7 +155,9 @@ def tile_picked_hashgmaxnorm2_none_po_kernel(
             product(y_banks[t][:], w1_dealt, w1s_dealt, t, x_picked[:], xs_plane[:])
         for c in range(2):
             nc.scalar.activation(sig[0][:, cols(c)], y0_banks[c][:, :HALF], ACT.Sigmoid)
-            nc.vector.tensor_copy(y[0][:, cols(1 - c)], y0_banks[1 - c][:, :HALF])
+            nc.vector.tensor_scalar(
+                y[0][:, cols(1 - c)], y0_banks[1 - c][:, :HALF], gain_size[:, 0:1], None, ALU.mult
+            )
 
         def gate(t, c):
             nc.vector.tensor_tensor(
@@ -152,29 +165,42 @@ def tile_picked_hashgmaxnorm2_none_po_kernel(
             )
 
         def fetch_other(t, c):
-            nc.scalar.activation(other[c][:, t, :], y[t][:].indirect(entries(lists["n2"], c)), ACT.Copy)
+            if (t, c) in OTHER_ON_VECTOR:
+                nc.vector.tensor_copy(other[c][:, t, :], y[t][:].indirect(entries(lists["n2"], c)))
+            else:
+                nc.scalar.activation(other[c][:, t, :], y[t][:].indirect(entries(lists["n2"], c)), ACT.Copy)
 
-        def take_larger(pair, c):
-            ts = slice(2 * pair, 2 * pair + 2)
-            nc.vector.tensor_tensor(larger[c][:, ts, :], gated[c][:, ts, :], other[c][:, ts, :], ALU.max)
-
-        def scale_and_round(c):
+        def take_larger(c, span):
             nc.vector.tensor_tensor(
-                z_bf[c][:].rearrange("p (g i) t -> p g t i", i=4),
-                larger[c][:].rearrange("p t (g i) -> p g t i", i=4),
-                gain[:].unsqueeze(1).unsqueeze(3).to_broadcast([P, HALF // 4, PACK, 4]),
-                ALU.mult,
+                larger[c][:, span, :].rearrange("p (g i) t -> p g t i", i=4),
+                gated[c][:, :, span].rearrange("p t (g i) -> p g t i", i=4),
+                other[c][:, :, span].rearrange("p t (g i) -> p g t i", i=4),
+                ALU.max,
             )
 
-        def quantize_z(c):
+        def apply_sign(c, span):
+            nc.vector.tensor_tensor(z_bf[c][:, span, :], larger[c][:, span, :], gain_sign[:, span, :], ALU.mult)
+
+        def quantize_z(c, span):
             nc.vector.quantize_mx(
-                out=z_codes[c][:].bitcast(FP8X4), scales=z_plane[c][:], in_=z_bf[c][:].rearrange("p j t -> p (j t)")
+                out=z_codes[c][:, span].bitcast(FP8X4),
+                scales=z_plane[c][:, span],
+                in_=z_bf[c][:, span, :].rearrange("p j t -> p (j t)"),
             )
+
+        def finish_z(c):
+            spans = [slice(b * HALF // ZS, (b + 1) * HALF // ZS) for b in range(ZS)]
+            for stage in (take_larger, apply_sign, quantize_z):
+                for span in spans:
+                    stage(c, span)
 
         for t in range(PACK):
             if t > 0:
-                nc.scalar.copy(y[t][:], y_banks[t][:])
+                if t not in Y_ON_VECTOR:
+                    nc.scalar.activation(y[t][:], y_banks[t][:], ACT.Copy, scale=gain_size[:, t : t + 1])
                 nc.scalar.activation(sig[t][:], y_banks[t][:], ACT.Sigmoid)
+                if t in Y_ON_VECTOR:
+                    nc.vector.tensor_scalar(y[t][:], y_banks[t][:], gain_size[:, t : t + 1], None, ALU.mult)
                 fetch_other(t - 1, 0)
             gate(t, 0)
             if t < PACK - 1:
@@ -183,7 +209,7 @@ def tile_picked_hashgmaxnorm2_none_po_kernel(
         for t in range(PACK):
             fetch_other(t, 1)
         if WARM:
-            nc.scalar.activation(warm[:, 2:3], other[1][:, PACK - 1, 0:1], ACT.Abs_reciprocal_sqrt, bias=0.5, scale=0.0)
+            nc.scalar.activation(warm[:, 2:3], other[1][:, WARM_T, 0:1], ACT.Abs_reciprocal_sqrt, bias=0.5, scale=0.0)
 
         h = [sb("h%d" % t, [P, S], F32) for t in range(2)]
         size = [sb("size%d" % t, [P, S], F32) for t in range(PACK)]
@@ -191,7 +217,7 @@ def tile_picked_hashgmaxnorm2_none_po_kernel(
         root = [sb("root%d" % c, [P, PACK, HALF], F32) for c in range(2)]
         inverse = [sb("inverse%d" % c, [P, PACK, HALF], F32) for c in range(2)]
         result = [sb("result%d" % c, [P, PACK, HALF], F32) for c in range(2)]
-        out_bf = [sb("out_bf%d" % c, [P, HALF, PACK], BF16) for c in range(2)]
+        out_bf = []
         out_codes = sb("out_codes", [P, S], U32)
         out_plane = sb("out_plane", [P, S], U8)
 
@@ -202,18 +228,12 @@ def tile_picked_hashgmaxnorm2_none_po_kernel(
                 h_banks[t, c] = bank(t + 4 * (1 - c))
                 product(h_banks[t, c][:, :HALF], w2_dealt, w2s_dealt, t, z_codes[c][:], z_plane[c][:])
 
-        take_larger(0, 0)
-        take_larger(1, 0)
-        scale_and_round(0)
+        finish_z(0)
         gate(PACK - 1, 1)
-        quantize_z(0)
         second_product(0)
         for t in range(PACK):
             nc.scalar.activation(size[t][:, cols(0)], h_banks[t, 0][:, :HALF], ACT.Abs)
-        take_larger(0, 1)
-        take_larger(1, 1)
-        scale_and_round(1)
-        quantize_z(1)
+        finish_z(1)
         second_product(1)
         h.append(sb("h2", [P, S], F32, tag="larger1"))
         h.append(sb("h3", [P, S], F32, tag="z_bf1"))
@@ -230,7 +250,7 @@ def tile_picked_hashgmaxnorm2_none_po_kernel(
                 nc.vector.tensor_copy(part[c][:, t, :], window)
 
         def invert(t0, c):
-            sums = bank(4 + (t0 // G) % 2)
+            sums = bank(SUMS + (t0 // G) % 2)
             for t in range(t0, t0 + G):
                 for b in range(HALF // P):
                     block = slice(b * P, (b + 1) * P)
@@ -246,7 +266,7 @@ def tile_picked_hashgmaxnorm2_none_po_kernel(
             )
 
         def turn_back(t0, c):
-            roots = bank(6 + (t0 // G) % 2)
+            roots = bank(10 - SUMS + (t0 // G) % 2)
             for t in range(t0, t0 + G):
                 for b in range(HALF // P):
                     block = slice(b * P, (b + 1) * P)
@@ -262,26 +282,33 @@ def tile_picked_hashgmaxnorm2_none_po_kernel(
             else:
                 nc.scalar.copy(h[t][:, cols(c)], h_banks[t, c][:, :HALF])
 
-        def divide(t, c):
+        def divide(t, lo, hi):
+            c, span = lo // HALF, slice(lo % HALF, lo % HALF + hi - lo)
             nc.vector.tensor_tensor(
-                result[c][:, t, :], h[t][:].indirect(entries(lists["n3"], c)), inverse[c][:, t, :], ALU.mult
+                result[c][:, t, span],
+                h[t][:].indirect(lists["n3"][:, lo // GROUP : hi // GROUP]),
+                inverse[c][:, t, span],
+                ALU.mult,
             )
+
+        def store(t, c):
             nc.sync.dma_start(out_rows[:, t, cols(c)], result[c][:, t, :])
 
-        def round_out(c):
-            nc.vector.tensor_copy(
-                out_bf[c][:].rearrange("p (g i) t -> p g t i", i=4), result[c][:].rearrange("p t (g i) -> p g t i", i=4)
+        def round_out(copy, lo, hi):
+            c, span = lo // HALF, slice(lo % HALF, lo % HALF + hi - lo)
+            copy(
+                out_bf[c][:, span, :].rearrange("p (g i) t -> p g t i", i=4),
+                result[c][:, :, span].rearrange("p t (g i) -> p g t i", i=4),
             )
 
-        def quantize_out(c):
+        def quantize_out(lo, hi):
+            c, span = lo // HALF, slice(lo % HALF, lo % HALF + hi - lo)
             nc.vector.quantize_mx(
-                out=out_codes[:, cols(c)].bitcast(FP8X4),
-                scales=out_plane[:, cols(c)],
-                in_=out_bf[c][:].rearrange("p j t -> p (j t)"),
+                out=out_codes[:, lo:hi].bitcast(FP8X4),
+                scales=out_plane[:, lo:hi],
+                in_=out_bf[c][:, span, :].rearrange("p j t -> p (j t)"),
             )
-            nc.sync.dma_start(
-                out_1[0].rearrange("p n t -> p (n t)").bitcast(I32)[:, cols(c)], out_codes[:, cols(c)].bitcast(I32)
-            )
+            nc.sync.dma_start(out_1[0].rearrange("p n t -> p (n t)").bitcast(I32)[:, lo:hi], out_codes[:, lo:hi].bitcast(I32))
 
         for t in range(PACK):
             nc.scalar.activation(size[t][:, cols(1)], h_banks[t, 1][:, :HALF], ACT.Abs)
@@ -299,15 +326,36 @@ def tile_picked_hashgmaxnorm2_none_po_kernel(
                     copy_h(t, 1)
                     fetch_size(t, 1)
             if 2 <= step:
-                t0, c = pieces[step - 2]
-                for t in range(t0, t0 + G):
-                    divide(t, c)
-            if step == PACK // G + 2:
-                round_out(0)
-            if step == PACK // G + 3:
-                quantize_out(0)
-        round_out(1)
-        quantize_out(1)
+                t, c = pieces[step - 2]
+                if SPLIT == 2 and (t, c) == (PACK - 1, 1):
+                    continue
+                divide(t, c * HALF, (c + 1) * HALF)
+                store(t, c)
+            if step == PACK + 2 and ROUND0 == 0:
+                out_bf.append(sb("out_bf0", [P, HALF, PACK], BF16))
+                round_out(nc.vector.tensor_copy, 0, HALF)
+            if step == PACK + 3 and ROUND0 == 0:
+                quantize_out(0, HALF)
+        if ROUND0 == 1:
+            out_bf.append(sb("out_bf0", [P, HALF, PACK], BF16, tag="root1"))
+            round_out(nc.scalar.copy, 0, HALF)
+        out_bf.append(sb("out_bf1", [P, HALF, PACK], BF16))
+        if SPLIT == 2:
+            mid = HALF + HALF // 2
+            divide(PACK - 1, HALF, mid)
+            divide(PACK - 1, mid, S)
+            store(PACK - 1, 1)
+            round_out(nc.vector.tensor_copy, HALF, mid)
+            round_out(nc.vector.tensor_copy, mid, S)
+            quantize_out(HALF, mid)
+            if ROUND0 == 1:
+                quantize_out(0, HALF)
+            quantize_out(mid, S)
+        else:
+            round_out(nc.vector.tensor_copy, HALF, S)
+            if ROUND0 == 1:
+                quantize_out(0, HALF)
+            quantize_out(HALF, S)
         for q in range(4):
             queue = nc.sync if q % 2 == 0 else nc.scalar
             queue.dma_start(out_2[0, 4 * q : 4 * q + 4, :].bitcast(I32), out_plane[32 * q : 32 * q + 4, :].bitcast(I32))

from contextlib import ExitStack

import concourse.mybir as mybir
from concourse.masks import make_identity

K, T, S, N, H = 512, 2048, 512, 512, 512
FLOPS = 2 * K * H * S + 2 * H * N * S

F32 = mybir.dt.float32
BF16 = mybir.dt.bfloat16
I32 = mybir.dt.int32
U32 = mybir.dt.uint32
U16 = mybir.dt.uint16
U8 = mybir.dt.uint8
FP8X4 = mybir.dt.float8_e4m3fn_x4
FP4X4 = mybir.dt.float4_e2m1fn_x4
ALU = mybir.AluOpType
ACT = mybir.ActivationFunctionType

P = 128
PACK = 4
HALF = S // 2
GROUP = 16
ZS = 2
Y_ON_VECTOR = []
OTHER_ON_VECTOR = [(3, 0)]
WARM_T = 3
SUMS = 6
SPLIT = 2
ROUND0 = 0
G = 1
H_ON_VECTOR = []
WARM = True
ON_SCALAR = [(3, 1)]


def tile_picked_hashgmaxnorm2_none_po_kernel(
    tc, x_words, x_scales, w1_words, w1_scales, gn, w2_words, w2_scales, offs, n1, n2, n3, n4, out_0, out_1, out_2
):
    nc = tc.nc
    with ExitStack() as ctx:
        held = ctx.enter_context(tc.tile_pool(name="held", bufs=1))
        psum = ctx.enter_context(tc.psum_pool(name="psum", bufs=1))

        def sb(name, shape, dtype, tag=None):
            return held.tile(shape, dtype, name=name, tag=tag or name, align_bytes=64)

        def cols(c):
            return slice(c * HALF, (c + 1) * HALF)

        def entries(lst, c):
            return lst[:, c * HALF // GROUP : (c + 1) * HALF // GROUP]

        lists = {}
        for name in ("offs", "n1", "n2", "n3", "n4"):
            lists[name] = held.tile([P, S // GROUP], U16, name="list_" + name)

        x_table = sb("x_table", [P, T], I32)
        xs_table = sb("xs_table", [P, T], U8)
        xs_picked = sb("xs_picked", [P, S], U8)
        xs_plane = sb("xs_plane", [P, S], U8)
        w_raw = sb("w_raw", [P, 2 * H], U8)
        ws_raw = sb("ws_raw", [P, H], U8)
        w1_dealt = sb("w1_dealt", [P, 2 * H], U8)
        w1s_dealt = sb("w1s_dealt", [P, H], U8)
        gain = sb("gain", [P, PACK], F32)

        w2_raw = sb("w2_raw", [P, 2 * N], U8)
        identity = sb("identity", [P, P], F32)

        w2_dealt = sb("w2_dealt", [P, 2 * N], U8)
        ws2_raw = sb("ws2_raw", [P, N], U8)
        w2s_dealt = sb("w2s_dealt", [P, N], U8)

        def load_scale_rows(queue, raw, src):
            for q in range(4):
                queue[q].dma_start(raw[32 * q : 32 * q + 4, :].bitcast(I32), src[0, 4 * q : 4 * q + 4, :].bitcast(I32))

        def deal_words(dst, raw):
            nc.scalar.copy(
                dst[:].bitcast(U16).rearrange("p (t m) -> p t m", t=PACK),
                raw[:].bitcast(U16).rearrange("p (m t) -> p t m", t=PACK),
            )

        def deal_scales(engine, dst, raw):
            engine.tensor_copy(
                dst[:].rearrange("p (t m) -> p t m", t=PACK), raw[:].rearrange("p (m t) -> p t m", t=PACK)
            )

        nc.vector.memset(xs_table[:].bitcast(I32), 0)
        nc.vector.memset(ws_raw[:].bitcast(I32), 0)
        nc.sync.dma_start(lists["offs"][:], offs)
        nc.sync.dma_start(xs_table[0:P:8, :].bitcast(I32), x_scales[0].bitcast(I32))
        nc.sync.dma_start(lists["n1"][:], n1)
        nc.sync.dma_start(lists["n2"][:], n2)
        nc.sync.dma_start(x_table[:], x_words[0].rearrange("p n t -> p (n t)").bitcast(I32))
        load_scale_rows([nc.scalar] * 4, ws_raw, w1_scales)
        nc.gpsimd.dma_start(w_raw[:].bitcast(I32), w1_words[0].bitcast(I32))
        nc.gpsimd.dma_start(gain[:], gn.rearrange("(p t) o -> p (t o)", t=PACK))
        nc.gpsimd.dma_start(w2_raw[:].bitcast(I32), w2_words[0].bitcast(I32))
        nc.gpsimd.memset(ws2_raw[:].bitcast(I32), 0)
        load_scale_rows([nc.gpsimd] * 4, ws2_raw, w2_scales)
        make_identity(nc, identity[:])
        warm = sb("warm", [P, 3], F32)
        if WARM:
            nc.vector.memset(warm[:, 0:1], 0.0)
            nc.scalar.activation(warm[:, 1:2], warm[:, 0:1], ACT.Sigmoid)

        nc.vector.tensor_copy(xs_picked[:], xs_table[:].indirect(lists["offs"][:]))
        nc.vector.tensor_copy(xs_plane[:].bitcast(I32), xs_picked[:].bitcast(I32))
        for j in range(1, 4):
            nc.sync.dma_start(xs_plane[j:P:32, :].bitcast(I32), xs_picked[8 * j : P : 32, :].bitcast(I32))
        nc.sync.dma_start(lists["n3"][:], n3)
        nc.sync.dma_start(lists["n4"][:], n4)
        deal_words(w1_dealt, w_raw)
        gain_size = sb("gain_size", [P, PACK], F32)
        gain_sign = sb("gain_sign", [P, HALF, PACK], BF16)
        nc.scalar.activation(gain_size[:], gain[:], ACT.Abs)
        nc.scalar.activation(gain_sign[:], gain[:].unsqueeze(1).to_broadcast([P, HALF, PACK]), ACT.Sign)
        deal_scales(nc.vector, w1s_dealt, ws_raw)
        x_picked = sb("x_picked", [P, S], U32, tag="ws_raw")
        nc.vector.tensor_copy(x_picked[:], x_table[:].bitcast(U32).indirect(lists["offs"][:]))
        deal_words(w2_dealt, w2_raw)
        deal_scales(nc.gpsimd, w2s_dealt, ws2_raw)

        def product(out, words, scales, t, codes, plane):
            nc.tensor.matmul_mx(
                out=out,
                lhsT=words[:, 2 * P * t : 2 * P * (t + 1)].bitcast(FP4X4),
                lhsT_scale=scales[:, P * t : P * (t + 1)],
                rhs=codes.bitcast(FP8X4),
                rhs_scale=plane,
                start=True,
                stop=True,
            )

        def bank(b):
            return psum.tile([P, S], F32, name="bank%d" % b, tag="bank%d" % b)

        y = [sb("y%d" % t, [P, S], F32) for t in range(PACK)]
        sig = [sb("sig%d" % t, [P, S], F32) for t in range(PACK)]
        gated = [sb("gated%d" % c, [P, PACK, HALF], F32) for c in range(2)]
        other = [sb("other%d" % c, [P, PACK, HALF], F32) for c in range(2)]
        larger = [sb("larger1", [P, HALF, PACK], BF16)] * 2
        z_bf = [sb("z_bf%d" % c, [P, HALF, PACK], BF16) for c in range(2)]
        z_codes = [sb("z_codes%d" % c, [P, HALF], U32) for c in range(2)]
        z_plane = [sb("z_plane%d" % c, [P, HALF], U8) for c in range(2)]

        y0_banks = [bank(0), bank(4)]
        for c in range(2):
            product(y0_banks[c][:, :HALF], w1_dealt, w1s_dealt, 0, x_picked[:, cols(c)], xs_plane[:, cols(c)])
        y_banks = [None]
        for t in range(1, PACK):
            y_banks.append(bank(t))
            product(y_banks[t][:], w1_dealt, w1s_dealt, t, x_picked[:], xs_plane[:])
        for c in range(2):
            nc.scalar.activation(sig[0][:, cols(c)], y0_banks[c][:, :HALF], ACT.Sigmoid)
            nc.vector.tensor_scalar(
                y[0][:, cols(1 - c)], y0_banks[1 - c][:, :HALF], gain_size[:, 0:1], None, ALU.mult
            )

        def gate(t, c):
            nc.vector.tensor_tensor(
                gated[c][:, t, :], sig[t][:].indirect(entries(lists["n1"], c)), y[t][:, cols(c)], ALU.mult
            )

        def fetch_other(t, c):
            if (t, c) in OTHER_ON_VECTOR:
                nc.vector.tensor_copy(other[c][:, t, :], y[t][:].indirect(entries(lists["n2"], c)))
            else:
                nc.scalar.activation(other[c][:, t, :], y[t][:].indirect(entries(lists["n2"], c)), ACT.Copy)

        def take_larger(c, span):
            nc.vector.tensor_tensor(
                larger[c][:, span, :].rearrange("p (g i) t -> p g t i", i=4),
                gated[c][:, :, span].rearrange("p t (g i) -> p g t i", i=4),
                other[c][:, :, span].rearrange("p t (g i) -> p g t i", i=4),
                ALU.max,
            )

        def apply_sign(c, span):
            nc.vector.tensor_tensor(z_bf[c][:, span, :], larger[c][:, span, :], gain_sign[:, span, :], ALU.mult)

        def quantize_z(c, span):
            nc.vector.quantize_mx(
                out=z_codes[c][:, span].bitcast(FP8X4),
                scales=z_plane[c][:, span],
                in_=z_bf[c][:, span, :].rearrange("p j t -> p (j t)"),
            )

        def finish_z(c):
            spans = [slice(b * HALF // ZS, (b + 1) * HALF // ZS) for b in range(ZS)]
            for stage in (take_larger, apply_sign, quantize_z):
                for span in spans:
                    stage(c, span)

        for t in range(PACK):
            if t > 0:
                if t not in Y_ON_VECTOR:
                    nc.scalar.activation(y[t][:], y_banks[t][:], ACT.Copy, scale=gain_size[:, t : t + 1])
                nc.scalar.activation(sig[t][:], y_banks[t][:], ACT.Sigmoid)
                if t in Y_ON_VECTOR:
                    nc.vector.tensor_scalar(y[t][:], y_banks[t][:], gain_size[:, t : t + 1], None, ALU.mult)
                fetch_other(t - 1, 0)
            gate(t, 0)
            if t < PACK - 1:
                gate(t, 1)
        fetch_other(PACK - 1, 0)
        for t in range(PACK):
            fetch_other(t, 1)
        if WARM:
            nc.scalar.activation(warm[:, 2:3], other[1][:, WARM_T, 0:1], ACT.Abs_reciprocal_sqrt, bias=0.5, scale=0.0)

        h = [sb("h%d" % t, [P, S], F32) for t in range(2)]
        size = [sb("size%d" % t, [P, S], F32) for t in range(PACK)]
        part = [sb("part", [P, PACK, HALF], F32)] * 2
        root = [sb("root%d" % c, [P, PACK, HALF], F32) for c in range(2)]
        inverse = [sb("inverse%d" % c, [P, PACK, HALF], F32) for c in range(2)]
        result = [sb("result%d" % c, [P, PACK, HALF], F32) for c in range(2)]
        out_bf = []
        out_codes = sb("out_codes", [P, S], U32)
        out_plane = sb("out_plane", [P, S], U8)

        h_banks = {}

        def second_product(c):
            for t in range(PACK):
                h_banks[t, c] = bank(t + 4 * (1 - c))
                product(h_banks[t, c][:, :HALF], w2_dealt, w2s_dealt, t, z_codes[c][:], z_plane[c][:])

        finish_z(0)
        gate(PACK - 1, 1)
        second_product(0)
        for t in range(PACK):
            nc.scalar.activation(size[t][:, cols(0)], h_banks[t, 0][:, :HALF], ACT.Abs)
        finish_z(1)
        second_product(1)
        h.append(sb("h2", [P, S], F32, tag="larger1"))
        h.append(sb("h3", [P, S], F32, tag="z_bf1"))
        for t in range(2, PACK):
            nc.vector.tensor_copy(h[t][:, cols(0)], h_banks[t, 0][:, :HALF])

        out_rows = out_0.rearrange("(p t) j -> p t j", t=PACK)

        def fetch_size(t, c):
            window = size[t][:].indirect(entries(lists["n4"], c))
            if (t, c) in ON_SCALAR:
                nc.scalar.activation(part[c][:, t, :], window, ACT.Copy)
            else:
                nc.vector.tensor_copy(part[c][:, t, :], window)

        def invert(t0, c):
            sums = bank(SUMS + (t0 // G) % 2)
            for t in range(t0, t0 + G):
                for b in range(HALF // P):
                    block = slice(b * P, (b + 1) * P)
                    place = slice((t - t0) * HALF + b * P, (t - t0) * HALF + (b + 1) * P)
                    nc.tensor.matmul(
                        sums[:, place], part[c][:, t, block], identity[:], start=True, stop=False, is_transpose=True
                    )
                    nc.tensor.matmul(
                        sums[:, place], size[t][:, cols(c)][:, block], identity[:], start=False, stop=True, is_transpose=True
                    )
            nc.scalar.activation(
                root[c][:, t0 : t0 + G, :].rearrange("p t j -> p (t j)"), sums[:, : G * HALF], ACT.Abs_reciprocal_sqrt, bias=0.5
            )

        def turn_back(t0, c):
            roots = bank(10 - SUMS + (t0 // G) % 2)
            for t in range(t0, t0 + G):
                for b in range(HALF // P):
                    block = slice(b * P, (b + 1) * P)
                    place = slice((t - t0) * HALF + b * P, (t - t0) * HALF + (b + 1) * P)
                    nc.tensor.transpose(roots[:, place], root[c][:, t, block], identity[:])
            nc.scalar.activation(
                inverse[c][:, t0 : t0 + G, :].rearrange("p t j -> p (t j)"), roots[:, : G * HALF], ACT.Square
            )

        def copy_h(t, c):
            if (t, c) in H_ON_VECTOR:
                nc.vector.tensor_copy(h[t][:, cols(c)], h_banks[t, c][:, :HALF])
            else:
                nc.scalar.copy(h[t][:, cols(c)], h_banks[t, c][:, :HALF])

        def divide(t, lo, hi):
            c, span = lo // HALF, slice(lo % HALF, lo % HALF + hi - lo)
            nc.vector.tensor_tensor(
                result[c][:, t, span],
                h[t][:].indirect(lists["n3"][:, lo // GROUP : hi // GROUP]),
                inverse[c][:, t, span],
                ALU.mult,
            )

        def store(t, c):
            nc.sync.dma_start(out_rows[:, t, cols(c)], result[c][:, t, :])

        def round_out(copy, lo, hi):
            c, span = lo // HALF, slice(lo % HALF, lo % HALF + hi - lo)
            copy(
                out_bf[c][:, span, :].rearrange("p (g i) t -> p g t i", i=4),
                result[c][:, :, span].rearrange("p t (g i) -> p g t i", i=4),
            )

        def quantize_out(lo, hi):
            c, span = lo // HALF, slice(lo % HALF, lo % HALF + hi - lo)
            nc.vector.quantize_mx(
                out=out_codes[:, lo:hi].bitcast(FP8X4),
                scales=out_plane[:, lo:hi],
                in_=out_bf[c][:, span, :].rearrange("p j t -> p (j t)"),
            )
            nc.sync.dma_start(out_1[0].rearrange("p n t -> p (n t)").bitcast(I32)[:, lo:hi], out_codes[:, lo:hi].bitcast(I32))

        for t in range(PACK):
            nc.scalar.activation(size[t][:, cols(1)], h_banks[t, 1][:, :HALF], ACT.Abs)
            fetch_size(t, 0)
            if t < 2:
                copy_h(t, 0)
        pieces = [(t, c) for c in range(2) for t in range(0, PACK, G)]
        for step in range(len(pieces) + 2):
            if step < len(pieces):
                invert(*pieces[step])
            if 1 <= step <= len(pieces):
                turn_back(*pieces[step - 1])
            if step < PACK // G:
                for t in range(step * G, (step + 1) * G):
                    copy_h(t, 1)
                    fetch_size(t, 1)
            if 2 <= step:
                t, c = pieces[step - 2]
                if SPLIT == 2 and (t, c) == (PACK - 1, 1):
                    continue
                divide(t, c * HALF, (c + 1) * HALF)
                store(t, c)
            if step == PACK + 2 and ROUND0 == 0:
                out_bf.append(sb("out_bf0", [P, HALF, PACK], BF16))
                round_out(nc.vector.tensor_copy, 0, HALF)
            if step == PACK + 3 and ROUND0 == 0:
                quantize_out(0, HALF)
        if ROUND0 == 1:
            out_bf.append(sb("out_bf0", [P, HALF, PACK], BF16, tag="root1"))
            round_out(nc.scalar.copy, 0, HALF)
        out_bf.append(sb("out_bf1", [P, HALF, PACK], BF16))
        if SPLIT == 2:
            mid = HALF + HALF // 2
            divide(PACK - 1, HALF, mid)
            divide(PACK - 1, mid, S)
            store(PACK - 1, 1)
            round_out(nc.vector.tensor_copy, HALF, mid)
            round_out(nc.vector.tensor_copy, mid, S)
            quantize_out(HALF, mid)
            if ROUND0 == 1:
                quantize_out(0, HALF)
            quantize_out(mid, S)
        else:
            round_out(nc.vector.tensor_copy, HALF, S)
            if ROUND0 == 1:
                quantize_out(0, HALF)
            quantize_out(HALF, S)
        for q in range(4):
            queue = nc.sync if q % 2 == 0 else nc.scalar
            queue.dma_start(out_2[0, 4 * q : 4 * q + 4, :].bitcast(I32), out_plane[32 * q : 32 * q + 4, :].bitcast(I32))
